import numpy as np
import ml_dtypes


def mxq(x, axis, fmt="e4m3"):
    dtype, down = {"e4m3": (ml_dtypes.float8_e4m3fn, 7), "e5m2": (ml_dtypes.float8_e5m2, 14)}[fmt]
    v = np.moveaxis(np.asarray(x, np.float32).astype(ml_dtypes.bfloat16).astype(np.float64), axis, -1)
    blocks = v.reshape(v.shape[:-1] + (-1, 32))
    amax = np.abs(blocks).max(-1, keepdims=True)
    byte = np.maximum(np.where(amax > 0, np.frexp(amax)[1] - 1 + 127, 0) - down, 1)
    scale = np.exp2(byte - 127.0)
    codes = (blocks / scale).astype(np.float32).astype(dtype).astype(np.float64)
    return np.moveaxis((codes * scale).reshape(v.shape), -1, axis)


WIDE = False


def mx_kscale(k, group=512):
    if not WIDE:
        return np.ones(k)
    levels = np.array([10, -10, 5, -5, 0])
    if group != 512:
        return np.exp2(np.random.permutation(np.resize(levels, k // group))).repeat(group)
    if k % 512:
        return np.exp2(np.random.permutation(np.resize(levels, k // 32))).repeat(32)
    a = np.empty((k // 512, 16))
    for p in range(k // 512):
        a[p, :8] = np.random.permutation(np.resize(levels, 8))
        for g in range(8):
            far = levels[np.abs(levels - a[p, g]) >= 10]
            a[p, g + 8] = far[np.random.randint(len(far))]
    return np.exp2(a.ravel()).repeat(32)


def f64(x):
    return np.asarray(x).astype(np.float64)


def striped(idx):
    return np.tile(np.asarray(idx).reshape(-1, 16).T, (8, 1)).astype(np.uint16)


def unstriped(offs):
    return offs[:16].T.reshape(-1).astype(np.int64)


H, KV, D, NQ, N = 4, 1, 256, 512, 512


def setup_inputs():
    n = np.random.standard_normal
    s = mx_kscale(D, 0)[:, None]
    u = mx_kscale(N)
    t = np.random.uniform(0.5, 2.0, N) * u
    v = n((KV, N, 128))
    v[:, :, 127] = 1.0
    return {
        "qT": (n((H, D, NQ)) * s * (0.70 / np.sqrt(D))).astype(np.float32),
        "kT": (n((KV, D, N)) / s).astype(np.float32),
        "t": t.reshape(N, 1).astype(np.float32),
        "v": (v / t[:, None]).astype(np.float32),
        "kb": (0.5 * n((N, 1))).astype(np.float32),
        "mask": (np.arange(N)[:, None] <= np.sort(np.random.randint(N // 4, N, NQ))[None, :]).astype(np.float32),
        "og": n((H, NQ, 128)).astype(np.float32),
    }


def reference(qT, kT, t, v, kb, mask, og):
    a = np.repeat(mxq(f64(kT), 1, "e4m3"), H // KV, 0).transpose(0, 2, 1) @ mxq(f64(qT), 1, "e4m3")
    a = a + f64(kb)
    p = np.square(np.maximum(a, 0.0))
    p = p * f64(mask)
    w = p * f64(t)
    y = mxq(w, 1, "e4m3").transpose(0, 2, 1) @ np.repeat(mxq(f64(v), 1, "e4m3"), H // KV, 0)
    y = y / (y[:, :, 127:128] + 1.0)
    y = y / (1.0 + np.exp(-f64(og)))
    return y

@@ -1,0 +1,264 @@
+from contextlib import ExitStack
+
+import concourse.mybir as mybir
+
+H, D, NQ, NT, E = 4, 256, 512, 512, 128
+FLOPS = 2 * H * NQ * NT * (D + E)
+
+F32 = mybir.dt.float32
+BF16 = mybir.dt.bfloat16
+U32 = mybir.dt.uint32
+U8 = mybir.dt.uint8
+FP8X4 = mybir.dt.float8_e4m3fn_x4
+ALU = mybir.AluOpType
+ACT = mybir.ActivationFunctionType
+
+P = 128
+PACK = 4
+ROWS = 64
+QB = 128
+QW = 256
+RUN = 4
+F32_MAX = 3.4028234663852886e38
+
+
+def tile_rows_a_relu2_kb_mask_gate_kernel(tc, qT, kT, t, v, kb, mask, og, out):
+    nc = tc.nc
+    units = [(2 * pair + g, half) for pair in range(2) for half in range(2) for g in range(2)]
+    n_units = len(units)
+
+    with ExitStack() as ctx:
+        sb = ctx.enter_context(tc.tile_pool(name="sb", bufs=1))
+        ps = ctx.enter_context(tc.psum_pool(name="ps", bufs=1))
+        ctx.enter_context(tc.manual_schedule())
+
+        def tile(shape, dtype, name):
+            return sb.tile(shape, dtype, name=name, align_bytes=64)
+
+        def runs_out(x):
+            return x.rearrange("p (c i) j -> p c j i", i=RUN)
+
+        def runs_in(x):
+            return x.rearrange("p j (c i) -> p c j i", i=RUN)
+
+        def quantize(codes, scales, src):
+            nc.vector.quantize_mx(out=codes.bitcast(FP8X4), scales=scales, in_=src)
+
+        t_sb = tile([P, PACK], F32, "t_sb")
+        kb_sb = tile([P, PACK], F32, "kb_sb")
+        k_raw = tile([P, PACK, NT], F32, "k_raw")
+        v_raw = tile([P, PACK, E], F32, "v_raw")
+        q_raw = [tile([P, PACK, QW], F32, "q_raw%d" % c) for c in range(4)]
+        m_raw = [tile([P, PACK, QW], F32, "m_raw%d" % c) for c in range(2)]
+        og_raw = [tile([P, NQ // QB, E], F32, "og_raw%d" % h) for h in range(H)]
+
+        k_src = kT[0].rearrange("(p j) n -> p j n", j=PACK)
+        m_src = mask.rearrange("(p r) q -> p r q", r=PACK)
+
+        def load_q(c):
+            pair, half = divmod(c, 2)
+            src = qT[2 * pair : 2 * pair + 2].rearrange("g (p j) q -> (g p) j q", j=PACK)
+            nc.sync.dma_start(out=q_raw[c][:], in_=src[:, :, half * QW : (half + 1) * QW])
+
+        def load_mask(half):
+            nc.sync.dma_start(out=m_raw[half][:], in_=m_src[:, :, half * QW : (half + 1) * QW])
+
+        def load_og(h):
+            nc.sync.dma_start(out=og_raw[h][:], in_=og[h].rearrange("(c p) e -> p c e", p=P))
+
+        nc.scalar.dma_start(out=k_raw[ROWS:P], in_=k_src)
+        nc.sync.dma_start(out=t_sb[:], in_=t.rearrange("(p r) o -> p (r o)", r=PACK))
+        nc.sync.dma_start(out=k_raw[0:ROWS], in_=k_src)
+        load_q(0)
+        nc.sync.dma_start(out=kb_sb[:], in_=kb.rearrange("(p r) o -> p (r o)", r=PACK))
+        load_mask(0)
+        nc.sync.dma_start(out=v_raw[:], in_=v[0].rearrange("(p r) e -> p r e", r=PACK))
+        load_q(1)
+        load_mask(1)
+        load_og(0)
+        load_og(1)
+        load_q(2)
+        load_q(3)
+        load_og(2)
+        load_og(3)
+
+        zero = tile([P, PACK], F32, "zero")
+        half_exp = tile([P, PACK], F32, "half_exp")
+        t_abs = tile([P, PACK], F32, "t_abs")
+        t_sign = tile([P, PACK], F32, "t_sign")
+        t_root = tile([P, PACK], F32, "t_root")
+        nc.gpsimd.memset(zero[:], 0.0)
+        nc.scalar.activation(out=half_exp[:], in_=zero[:], func=ACT.Sigmoid)
+        nc.scalar.activation(out=t_abs[:], in_=t_sb[:], func=ACT.Abs)
+        nc.scalar.activation(out=t_sign[:], in_=t_sb[:], func=ACT.Sign)
+        nc.gpsimd.tensor_tensor(out=t_root[:], in0=t_abs[:], in1=half_exp[:], op=ALU.pow)
+
+        k_il = [tile([P, 2, P, PACK], BF16, "k_il%d" % i) for i in range(2)]
+        k_codes = [tile([P, 2 * P], U32, "k_codes%d" % i) for i in range(2)]
+        k_scales = [tile([P, 2 * P], U8, "k_scales%d" % i) for i in range(2)]
+        k_dealt = k_raw[:].rearrange("p j (s r) -> p r s j", r=PACK)
+        for r in range(2):
+            nc.vector.tensor_copy(out=k_il[0][:, r], in_=k_dealt[:, r])
+        for r in range(2):
+            nc.scalar.copy(out=k_il[1][:, r], in_=k_dealt[:, 2 + r])
+
+        def quantize_k(i):
+            quantize(k_codes[i][:], k_scales[i][:], k_il[i][:].rearrange("p r s j -> p (r s j)"))
+
+        q_il = [tile([P, QW, PACK], BF16, "q_il%d" % c) for c in range(4)]
+        q_codes = [tile([P, QW], U32, "q_codes%d" % c) for c in range(4)]
+        q_scales = [tile([P, QW], U8, "q_scales%d" % c) for c in range(4)]
+
+        def quantize_q(c):
+            quantize(q_codes[c][:], q_scales[c][:], q_il[c][:].rearrange("p q j -> p (q j)"))
+
+        gate_t = [tile([P, PACK, QW], F32, "mask_root%d" % c) for c in range(2)]
+
+        nc.vector.tensor_copy(out=runs_out(q_il[0][:]), in_=runs_in(q_raw[0][:]))
+        quantize_k(0)
+        quantize_q(0)
+        for r in range(PACK):
+            nc.scalar.activation(out=gate_t[0][:, r], in_=m_raw[0][:, r], func=ACT.Copy, scale=t_root[:, r : r + 1])
+        quantize_k(1)
+
+        v_il = tile([P, E, PACK], BF16, "v_il")
+        v_codes = tile([P, E], U32, "v_codes")
+        v_scales = tile([P, E], U8, "v_scales")
+        nc.gpsimd.tensor_tensor(
+            out=v_il[:],
+            in0=v_raw[:].rearrange("p r e -> p e r"),
+            in1=t_sign[:].unsqueeze(1).to_broadcast([P, E, PACK]),
+            op=ALU.mult,
+        )
+
+        banks, lin, pos, w_il, w_codes, w_scales, y_ps, den, rden, sig, res = ({} for i in range(11))
+
+        def scores(j):
+            h, half = units[j]
+            g, c = h % 2, 2 * (h // 2) + half
+            rows = slice(ROWS * g, ROWS * (g + 1))
+            banks[j] = []
+            for i in range(2):
+                bank = ps.tile([P, 2, QW], F32, name="s%d_%d" % (j, i), tag="scores%d" % g, bufs=3)
+                banks[j].append(bank)
+                for r in range(2):
+                    for b in range(QW // QB):
+                        tok = slice(P * r, P * (r + 1))
+                        cols = slice(QB * b, QB * (b + 1))
+                        nc.tensor.matmul_mx(
+                            out=bank[:, r, cols],
+                            lhsT=k_codes[i][rows, tok].bitcast(FP8X4),
+                            lhsT_scale=k_scales[i][rows, tok],
+                            rhs=q_codes[c][rows, cols].bitcast(FP8X4),
+                            rhs_scale=q_scales[c][rows, cols],
+                            start=True,
+                            stop=True,
+                        )
+
+        def bias_mask(j, r):
+            if r == 0:
+                lin[j] = tile([P, PACK, QW], F32, "lin%d" % j)
+                pos[j] = tile([P, PACK, QW], F32, "pos%d" % j)
+            nc.vector.scalar_tensor_tensor(
+                out=lin[j][:, r],
+                in0=banks[j][r // 2][:, r % 2],
+                scalar=kb_sb[:, r : r + 1],
+                in1=gate_t[units[j][1]][:, r],
+                op0=ALU.add,
+                op1=ALU.mult,
+            )
+
+        def relu(j, i):
+            nc.gpsimd.tensor_scalar(
+                out=pos[j][:, 2 * i : 2 * i + 2],
+                in0=lin[j][:, 2 * i : 2 * i + 2],
+                scalar1=F32_MAX,
+                scalar2=0.0,
+                op0=ALU.min,
+                op1=ALU.max,
+            )
+
+        def square(j):
+            w_il[j] = tile([P, QW, PACK], BF16, "w_il%d" % j)
+            nc.scalar.activation(out=runs_out(w_il[j][:]), in_=runs_in(pos[j][:]), func=ACT.Square)
+
+        def second_product(j):
+            w_codes[j] = tile([P, QW], U32, "w_codes%d" % j)
+            w_scales[j] = tile([P, QW], U8, "w_scales%d" % j)
+            quantize(w_codes[j][:], w_scales[j][:], w_il[j][:].rearrange("p q r -> p (q r)"))
+            y_ps[j] = ps.tile([P, QW // QB, E], F32, name="y%d" % j, tag="y", bufs=2)
+            for b in range(QW // QB):
+                cols = slice(QB * b, QB * (b + 1))
+                nc.tensor.matmul_mx(
+                    out=y_ps[j][:, b],
+                    lhsT=w_codes[j][:, cols].bitcast(FP8X4),
+                    lhsT_scale=w_scales[j][:, cols],
+                    rhs=v_codes[:].bitcast(FP8X4),
+                    rhs_scale=v_scales[:],
+                    start=True,
+                    stop=True,
+                )
+
+        def sigmoid(j):
+            h, half = units[j]
+            sig[j] = tile([P, QW // QB, E], F32, "sig%d" % j)
+            nc.scalar.activation(out=sig[j][:], in_=og_raw[h][:, 2 * half : 2 * half + 2], func=ACT.Sigmoid)
+
+        def denominator(j):
+            den[j] = tile([P, QW // QB], F32, "den%d" % j)
+            nc.vector.tensor_scalar_add(out=den[j][:], in0=y_ps[j][:, :, E - 1], scalar1=1.0)
+
+        def invert(j):
+            rden[j] = tile([P, QW // QB], F32, "rden%d" % j)
+            nc.vector.reciprocal(out=rden[j][:], in_=den[j][:])
+
+        def finish(j):
+            h, half = units[j]
+            res[j] = tile([P, QW // QB, E], F32, "res%d" % j)
+            for b in range(QW // QB):
+                nc.vector.scalar_tensor_tensor(
+                    out=res[j][:, b],
+                    in0=y_ps[j][:, b],
+                    scalar=rden[j][:, b : b + 1],
+                    in1=sig[j][:, b],
+                    op0=ALU.mult,
+                    op1=ALU.mult,
+                )
+            dst = out[h, half * QW : (half + 1) * QW].rearrange("(c p) e -> p c e", p=P)
+            nc.sync.dma_start(out=dst, in_=res[j][:])
+
+        scores(0)
+        for j in range(n_units + 2):
+            now, last, before = j < n_units, 0 <= j - 1 < n_units, j - 2 >= 0
+            if now:
+                bias_mask(j, 0)
+                bias_mask(j, 1)
+                relu(j, 0)
+            if j % 2 == 1 and j + 1 < n_units:
+                quantize_q((j + 1) // 2)
+            if j + 1 < n_units:
+                scores(j + 1)
+            if before:
+                denominator(j - 2)
+            if now:
+                bias_mask(j, 2)
+            if before:
+                invert(j - 2)
+            if now:
+                bias_mask(j, 3)
+                relu(j, 1)
+            if j == 0:
+                quantize(v_codes[:], v_scales[:], v_il[:].rearrange("p e r -> p (e r)"))
+            if j == 1:
+                for r in range(PACK):
+                    nc.vector.tensor_scalar_mul(out=gate_t[1][:, r], in0=m_raw[1][:, r], scalar1=t_root[:, r : r + 1])
+            if before:
+                finish(j - 2)
+            if last:
+                second_product(j - 1)
+            if now:
+                if j % 2 == 0 and j + 2 < n_units:
+                    c = j // 2 + 1
+                    nc.scalar.copy(out=runs_out(q_il[c][:]), in_=runs_in(q_raw[c][:]))
+                square(j)
+                sigmoid(j)

@@ -1,4 +1,5 @@
 from contextlib import ExitStack
+from functools import partial
 
 import concourse.mybir as mybir
 
@@ -9,6 +10,7 @@ F32 = mybir.dt.float32
 BF16 = mybir.dt.bfloat16
 U32 = mybir.dt.uint32
 U8 = mybir.dt.uint8
+I32 = mybir.dt.int32
 FP8X4 = mybir.dt.float8_e4m3fn_x4
 ALU = mybir.AluOpType
 ACT = mybir.ActivationFunctionType
@@ -19,13 +21,15 @@ ROWS = 64
 QB = 128
 QW = 256
 RUN = 4
+START = 3
+KW = 2 * P
 F32_MAX = 3.4028234663852886e38
+K_SPLIT = 80
 
 
 def tile_rows_a_relu2_kb_mask_gate_kernel(tc, qT, kT, t, v, kb, mask, og, out):
     nc = tc.nc
-    units = [(2 * pair + g, half) for pair in range(2) for half in range(2) for g in range(2)]
-    n_units = len(units)
+    n_steps = NQ // QW * (H // 2)
 
     with ExitStack() as ctx:
         sb = ctx.enter_context(tc.tile_pool(name="sb", bufs=1))
@@ -46,41 +50,33 @@ def tile_rows_a_relu2_kb_mask_gate_kernel(tc, qT, kT, t, v, kb, mask, og, out):
 
         t_sb = tile([P, PACK], F32, "t_sb")
         kb_sb = tile([P, PACK], F32, "kb_sb")
-        k_raw = tile([P, PACK, NT], F32, "k_raw")
+        k_raw = tile([ROWS, PACK, NT], F32, "k_raw")
         v_raw = tile([P, PACK, E], F32, "v_raw")
         q_raw = [tile([P, PACK, QW], F32, "q_raw%d" % c) for c in range(4)]
-        m_raw = [tile([P, PACK, QW], F32, "m_raw%d" % c) for c in range(2)]
+        m_raw = [[tile([P, 2, QW], F32, "m_raw%d_%d" % (c, i)) for i in range(2)] for c in range(2)]
         og_raw = [tile([P, NQ // QB, E], F32, "og_raw%d" % h) for h in range(H)]
 
         k_src = kT[0].rearrange("(p j) n -> p j n", j=PACK)
         m_src = mask.rearrange("(p r) q -> p r q", r=PACK)
 
         def load_q(c):
-            pair, half = divmod(c, 2)
+            half, pair = divmod(c, 2)
             src = qT[2 * pair : 2 * pair + 2].rearrange("g (p j) q -> (g p) j q", j=PACK)
             nc.sync.dma_start(out=q_raw[c][:], in_=src[:, :, half * QW : (half + 1) * QW])
 
         def load_mask(half):
-            nc.sync.dma_start(out=m_raw[half][:], in_=m_src[:, :, half * QW : (half + 1) * QW])
+            for i in range(2):
+                nc.sync.dma_start(out=m_raw[half][i][:], in_=m_src[:, 2 * i : 2 * i + 2, half * QW : (half + 1) * QW])
 
         def load_og(h):
             nc.sync.dma_start(out=og_raw[h][:], in_=og[h].rearrange("(c p) e -> p c e", p=P))
 
-        nc.scalar.dma_start(out=k_raw[ROWS:P], in_=k_src)
+        nc.scalar.dma_start(out=k_raw[:], in_=k_src)
+        nc.scalar.dma_start(out=kb_sb[:], in_=kb.rearrange("(p r) o -> p (r o)", r=PACK))
         nc.sync.dma_start(out=t_sb[:], in_=t.rearrange("(p r) o -> p (r o)", r=PACK))
-        nc.sync.dma_start(out=k_raw[0:ROWS], in_=k_src)
         load_q(0)
-        nc.sync.dma_start(out=kb_sb[:], in_=kb.rearrange("(p r) o -> p (r o)", r=PACK))
         load_mask(0)
-        nc.sync.dma_start(out=v_raw[:], in_=v[0].rearrange("(p r) e -> p r e", r=PACK))
         load_q(1)
-        load_mask(1)
-        load_og(0)
-        load_og(1)
-        load_q(2)
-        load_q(3)
-        load_og(2)
-        load_og(3)
 
         zero = tile([P, PACK], F32, "zero")
         half_exp = tile([P, PACK], F32, "half_exp")
@@ -88,22 +84,24 @@ def tile_rows_a_relu2_kb_mask_gate_kernel(tc, qT, kT, t, v, kb, mask, og, out):
         t_sign = tile([P, PACK], F32, "t_sign")
         t_root = tile([P, PACK], F32, "t_root")
         nc.gpsimd.memset(zero[:], 0.0)
+        k_mx = [tile([P, KW + KW // PACK], U32, "k_mx%d" % i) for i in range(2)]
+        for i in range(2):
+            nc.gpsimd.memset(k_mx[i][:, KW:], 0)
         nc.scalar.activation(out=half_exp[:], in_=zero[:], func=ACT.Sigmoid)
         nc.scalar.activation(out=t_abs[:], in_=t_sb[:], func=ACT.Abs)
         nc.scalar.activation(out=t_sign[:], in_=t_sb[:], func=ACT.Sign)
         nc.gpsimd.tensor_tensor(out=t_root[:], in0=t_abs[:], in1=half_exp[:], op=ALU.pow)
 
-        k_il = [tile([P, 2, P, PACK], BF16, "k_il%d" % i) for i in range(2)]
-        k_codes = [tile([P, 2 * P], U32, "k_codes%d" % i) for i in range(2)]
-        k_scales = [tile([P, 2 * P], U8, "k_scales%d" % i) for i in range(2)]
-        k_dealt = k_raw[:].rearrange("p j (s r) -> p r s j", r=PACK)
-        for r in range(2):
-            nc.vector.tensor_copy(out=k_il[0][:, r], in_=k_dealt[:, r])
-        for r in range(2):
-            nc.scalar.copy(out=k_il[1][:, r], in_=k_dealt[:, 2 + r])
+        k_il = tile([ROWS, PACK, P, PACK], BF16, "k_il")
+        k_codes = [k_mx[r // 2][:, P * (r % 2) : P * (r % 2 + 1)] for r in range(PACK)]
+        k_scales = [k_mx[r // 2][:, KW:].bitcast(U8)[:, P * (r % 2) : P * (r % 2 + 1)] for r in range(PACK)]
+        k_dst = k_il[:].rearrange("p r s j -> p s j r")
+        k_dealt = k_raw[:].rearrange("p j (s r) -> p s j r", r=PACK)
+        nc.vector.tensor_copy(out=k_dst[:, :K_SPLIT], in_=k_dealt[:, :K_SPLIT])
+        nc.scalar.copy(out=k_dst[:, K_SPLIT:], in_=k_dealt[:, K_SPLIT:])
 
-        def quantize_k(i):
-            quantize(k_codes[i][:], k_scales[i][:], k_il[i][:].rearrange("p r s j -> p (r s j)"))
+        def quantize_k(r):
+            quantize(k_codes[r][:ROWS], k_scales[r][:ROWS], k_il[:, r].rearrange("p s j -> p (s j)"))
 
         q_il = [tile([P, QW, PACK], BF16, "q_il%d" % c) for c in range(4)]
         q_codes = [tile([P, QW], U32, "q_codes%d" % c) for c in range(4)]
@@ -112,153 +110,231 @@ def tile_rows_a_relu2_kb_mask_gate_kernel(tc, qT, kT, t, v, kb, mask, og, out):
         def quantize_q(c):
             quantize(q_codes[c][:], q_scales[c][:], q_il[c][:].rearrange("p q j -> p (q j)"))
 
-        gate_t = [tile([P, PACK, QW], F32, "mask_root%d" % c) for c in range(2)]
+        def interleave_q(c, engine_copy):
+            engine_copy(out=runs_out(q_il[c][:]), in_=runs_in(q_raw[c][:]))
 
-        nc.vector.tensor_copy(out=runs_out(q_il[0][:]), in_=runs_in(q_raw[0][:]))
+        m_root = [tile([P, PACK, QW], F32, "m_root%d" % c) for c in range(2)]
+
+        def scale_mask_scalar(half, rs):
+            for r in rs:
+                src = m_raw[half][r // 2][:, r % 2]
+                nc.scalar.activation(out=m_root[half][:, r], in_=src, func=ACT.Copy, scale=t_root[:, r : r + 1])
+
+        def scale_mask_gpsimd(half):
+            for r in range(PACK):
+                src = m_raw[half][r // 2][:, r % 2]
+                nc.gpsimd.tensor_scalar(
+                    out=m_root[half][:, r], in0=src, scalar1=t_root[:, r : r + 1], scalar2=0.0, op0=ALU.mult, op1=ALU.add
+                )
+
+        lo, hi = slice(0, QB), slice(QB, QW)
+        nc.scalar.copy(out=runs_out(q_il[0][:, hi]), in_=runs_in(q_raw[0][:, :, hi]))
         quantize_k(0)
-        quantize_q(0)
-        for r in range(PACK):
-            nc.scalar.activation(out=gate_t[0][:, r], in_=m_raw[0][:, r], func=ACT.Copy, scale=t_root[:, r : r + 1])
         quantize_k(1)
+        nc.scalar.dma_start(out=k_mx[0][ROWS:].bitcast(I32), in_=k_mx[0][:ROWS].bitcast(I32))
+        nc.vector.tensor_copy(out=runs_out(q_il[0][:, lo]), in_=runs_in(q_raw[0][:, :, lo]))
+        quantize_k(2)
+        quantize_k(3)
+        quantize_q(0)
+        scale_mask_scalar(0, range(2))
+        nc.scalar.dma_start(out=k_mx[1][ROWS:].bitcast(I32), in_=k_mx[1][:ROWS].bitcast(I32))
+        scale_mask_scalar(0, range(2, 4))
+        load_q(2)
+        load_mask(1)
+        nc.sync.dma_start(out=v_raw[:], in_=v[0].rearrange("(p r) e -> p r e", r=PACK))
+        load_og(0)
+        load_q(3)
+        for h in range(1, H):
+            load_og(h)
 
         v_il = tile([P, E, PACK], BF16, "v_il")
         v_codes = tile([P, E], U32, "v_codes")
         v_scales = tile([P, E], U8, "v_scales")
-        nc.gpsimd.tensor_tensor(
-            out=v_il[:],
-            in0=v_raw[:].rearrange("p r e -> p e r"),
-            in1=t_sign[:].unsqueeze(1).to_broadcast([P, E, PACK]),
-            op=ALU.mult,
-        )
 
-        banks, lin, pos, w_il, w_codes, w_scales, y_ps, den, rden, sig, res = ({} for i in range(11))
+        def sign_v():
+            sign = t_sign[:].unsqueeze(1).unsqueeze(3).to_broadcast([P, E // RUN, PACK, RUN])
+            nc.vector.tensor_tensor(out=runs_out(v_il[:]), in0=runs_in(v_raw[:]), in1=sign, op=ALU.mult)
 
-        def scores(j):
-            h, half = units[j]
-            g, c = h % 2, 2 * (h // 2) + half
+        banks, lin, pos, w_sq, w_il, y_ps, den, rden, sig, res = ({} for i in range(10))
+        NB = QW // QB
+
+        def scores(c, g):
             rows = slice(ROWS * g, ROWS * (g + 1))
-            banks[j] = []
+            banks[c, g] = []
             for i in range(2):
-                bank = ps.tile([P, 2, QW], F32, name="s%d_%d" % (j, i), tag="scores%d" % g, bufs=3)
-                banks[j].append(bank)
+                bank = ps.tile([P, 2, QW], F32, name="s%d_%d_%d" % (c, g, i), tag="scores%d" % g, bufs=2)
                 for r in range(2):
-                    for b in range(QW // QB):
-                        tok = slice(P * r, P * (r + 1))
+                    banks[c, g].append(bank[:, r])
+                    for b in range(NB):
                         cols = slice(QB * b, QB * (b + 1))
                         nc.tensor.matmul_mx(
                             out=bank[:, r, cols],
-                            lhsT=k_codes[i][rows, tok].bitcast(FP8X4),
-                            lhsT_scale=k_scales[i][rows, tok],
+                            lhsT=k_codes[2 * i + r][rows].bitcast(FP8X4),
+                            lhsT_scale=k_scales[2 * i + r][rows],
                             rhs=q_codes[c][rows, cols].bitcast(FP8X4),
                             rhs_scale=q_scales[c][rows, cols],
                             start=True,
                             stop=True,
                         )
 
-        def bias_mask(j, r):
+        def bias_mask(c, g, r):
             if r == 0:
-                lin[j] = tile([P, PACK, QW], F32, "lin%d" % j)
-                pos[j] = tile([P, PACK, QW], F32, "pos%d" % j)
+                lin[c, g] = tile([P, PACK, QW], F32, "lin%d_%d" % (c, g))
+                pos[c, g] = tile([P, PACK, QW], F32, "pos%d_%d" % (c, g))
             nc.vector.scalar_tensor_tensor(
-                out=lin[j][:, r],
-                in0=banks[j][r // 2][:, r % 2],
+                out=lin[c, g][:, r],
+                in0=banks[c, g][r],
                 scalar=kb_sb[:, r : r + 1],
-                in1=gate_t[units[j][1]][:, r],
+                in1=m_root[c // 2][:, r],
                 op0=ALU.add,
                 op1=ALU.mult,
             )
 
-        def relu(j, i):
+        def relu_gpsimd(c, g):
             nc.gpsimd.tensor_scalar(
-                out=pos[j][:, 2 * i : 2 * i + 2],
-                in0=lin[j][:, 2 * i : 2 * i + 2],
-                scalar1=F32_MAX,
-                scalar2=0.0,
-                op0=ALU.min,
-                op1=ALU.max,
+                out=pos[c, g][:], in0=lin[c, g][:], scalar1=F32_MAX, scalar2=0.0, op0=ALU.min, op1=ALU.max
             )
 
-        def square(j):
-            w_il[j] = tile([P, QW, PACK], BF16, "w_il%d" % j)
-            nc.scalar.activation(out=runs_out(w_il[j][:]), in_=runs_in(pos[j][:]), func=ACT.Square)
+        def relu_vector(c, g, rs):
+            nc.vector.tensor_scalar_max(out=pos[c, g][:, rs], in0=lin[c, g][:, rs], scalar1=0.0)
 
-        def second_product(j):
-            w_codes[j] = tile([P, QW], U32, "w_codes%d" % j)
-            w_scales[j] = tile([P, QW], U8, "w_scales%d" % j)
-            quantize(w_codes[j][:], w_scales[j][:], w_il[j][:].rearrange("p q r -> p (q r)"))
-            y_ps[j] = ps.tile([P, QW // QB, E], F32, name="y%d" % j, tag="y", bufs=2)
-            for b in range(QW // QB):
+        def square(c, g, cols):
+            if cols.start == 0:
+                w_sq[c, g] = tile([P, QW, PACK], BF16, "w_sq%d_%d" % (c, g))
+            nc.scalar.activation(out=runs_out(w_sq[c, g][:, cols]), in_=runs_in(pos[c, g][:, :, cols]), func=ACT.Square)
+
+        def second_product(name, w, y):
+            multiply(*quantize_w(name, w), y)
+
+        def quantize_w(name, w):
+            width = w.shape[1]
+            codes = tile([P, width], U32, "w_codes" + name)
+            scales = tile([P, width], U8, "w_scales" + name)
+            quantize(codes[:], scales[:], w.rearrange("p q r -> p (q r)"))
+            return codes, scales
+
+        def multiply(codes, scales, y):
+            for b in range(y.shape[1]):
                 cols = slice(QB * b, QB * (b + 1))
                 nc.tensor.matmul_mx(
-                    out=y_ps[j][:, b],
-                    lhsT=w_codes[j][:, cols].bitcast(FP8X4),
-                    lhsT_scale=w_scales[j][:, cols],
+                    out=y[:, b],
+                    lhsT=codes[:, cols].bitcast(FP8X4),
+                    lhsT_scale=scales[:, cols],
                     rhs=v_codes[:].bitcast(FP8X4),
                     rhs_scale=v_scales[:],
                     start=True,
                     stop=True,
                 )
 
-        def sigmoid(j):
-            h, half = units[j]
-            sig[j] = tile([P, QW // QB, E], F32, "sig%d" % j)
-            nc.scalar.activation(out=sig[j][:], in_=og_raw[h][:, 2 * half : 2 * half + 2], func=ACT.Sigmoid)
+        def sigmoid(c, g):
+            h, half = 2 * (c % 2) + g, c // 2
+            sig[c, g] = tile([P, NB, E], F32, "sig%d_%d" % (c, g))
+            nc.scalar.activation(out=sig[c, g][:], in_=og_raw[h][:, NB * half : NB * (half + 1)], func=ACT.Sigmoid)
 
-        def denominator(j):
-            den[j] = tile([P, QW // QB], F32, "den%d" % j)
-            nc.vector.tensor_scalar_add(out=den[j][:], in0=y_ps[j][:, :, E - 1], scalar1=1.0)
+        def denominator(name, y):
+            den[name] = tile([P, y.shape[1]], F32, "den" + name)
+            nc.vector.tensor_scalar_add(out=den[name][:], in0=y[:, :, E - 1], scalar1=1.0)
 
-        def invert(j):
-            rden[j] = tile([P, QW // QB], F32, "rden%d" % j)
-            nc.vector.reciprocal(out=rden[j][:], in_=den[j][:])
+        def denominator_of(c):
+            denominator(str(c), y_ps[c][:])
 
-        def finish(j):
-            h, half = units[j]
-            res[j] = tile([P, QW // QB, E], F32, "res%d" % j)
-            for b in range(QW // QB):
+        def invert(name):
+            rden[name] = tile([P, den[name].shape[1]], F32, "rden" + name)
+            nc.vector.reciprocal(out=rden[name][:], in_=den[name][:])
+
+        def finish(c, g, blocks, y, inv):
+            h, q0 = 2 * (c % 2) + g, (c // 2) * QW + blocks[0] * QB
+            result = tile([P, len(blocks), E], F32, "res%d_%d_%d" % (c, g, blocks[0]))
+            for i, b in enumerate(blocks):
                 nc.vector.scalar_tensor_tensor(
-                    out=res[j][:, b],
-                    in0=y_ps[j][:, b],
-                    scalar=rden[j][:, b : b + 1],
-                    in1=sig[j][:, b],
-                    op0=ALU.mult,
-                    op1=ALU.mult,
+                    out=result[:, i], in0=y[:, i], scalar=inv[:, i : i + 1], in1=sig[c, g][:, b], op0=ALU.mult, op1=ALU.mult
                 )
-            dst = out[h, half * QW : (half + 1) * QW].rearrange("(c p) e -> p c e", p=P)
-            nc.sync.dma_start(out=dst, in_=res[j][:])
+            dst = out[h, q0 : q0 + len(blocks) * QB].rearrange("(c p) e -> p c e", p=P)
+            nc.sync.dma_start(out=dst, in_=result[:])
 
-        scores(0)
-        for j in range(n_units + 2):
-            now, last, before = j < n_units, 0 <= j - 1 < n_units, j - 2 >= 0
-            if now:
-                bias_mask(j, 0)
-                bias_mask(j, 1)
-                relu(j, 0)
-            if j % 2 == 1 and j + 1 < n_units:
-                quantize_q((j + 1) // 2)
-            if j + 1 < n_units:
-                scores(j + 1)
-            if before:
-                denominator(j - 2)
-            if now:
-                bias_mask(j, 2)
-            if before:
-                invert(j - 2)
-            if now:
-                bias_mask(j, 3)
-                relu(j, 1)
-            if j == 0:
+        def y_bank(name, blocks):
+            return ps.tile([P, blocks, E], F32, name="y" + name, tag="y", bufs=4)
+
+        whole = slice(0, QW)
+        n_units = 2 * n_steps
+        last = n_units - 1
+
+        def product(j):
+            c, g = divmod(j, 2)
+            if g == 0:
+                y_ps[c] = y_bank(str(c), 2 * NB)
+            second_product(str(j), w_sq[c, g][:], y_ps[c][:, NB * g : NB * (g + 1)])
+
+        def finish_unit(j):
+            c, g = divmod(j, 2)
+            finish(c, g, range(NB), y_ps[c][:, NB * g : NB * (g + 1)], rden[str(c)][:, NB * g : NB * (g + 1)])
+
+        back = [partial(product, 0), partial(product, 1)]
+        for c in range(n_steps - 1):
+            back.append(partial(denominator_of, c))
+            back.append(partial(product, 2 * c + 2))
+            back.append(partial(invert, str(c)))
+            if 2 * c + 3 < last:
+                back.append(partial(product, 2 * c + 3))
+            back.append(partial(finish_unit, 2 * c))
+            back.append(partial(finish_unit, 2 * c + 1))
+
+        scores(0, 0)
+        interleave_q(1, nc.scalar.copy)
+        interleave_q(2, nc.scalar.copy)
+        scale_mask_scalar(1, range(PACK))
+        for j in range(n_units):
+            c, g = divmod(j, 2)
+            if j < last:
+                scores(*divmod(j + 1, 2))
+            bias_mask(c, g, 0)
+            bias_mask(c, g, 1)
+            bias_mask(c, g, 2)
+            if j == last:
+                back.pop(0)()
+            bias_mask(c, g, 3)
+            if g == 0 and c + 1 < n_steps:
+                quantize_q(c + 1)
+            if j == 2:
+                sign_v()
+            if j == START:
                 quantize(v_codes[:], v_scales[:], v_il[:].rearrange("p e r -> p (e r)"))
-            if j == 1:
-                for r in range(PACK):
-                    nc.vector.tensor_scalar_mul(out=gate_t[1][:, r], in0=m_raw[1][:, r], scalar1=t_root[:, r : r + 1])
-            if before:
-                finish(j - 2)
-            if last:
-                second_product(j - 1)
-            if now:
-                if j % 2 == 0 and j + 2 < n_units:
-                    c = j // 2 + 1
-                    nc.scalar.copy(out=runs_out(q_il[c][:]), in_=runs_in(q_raw[c][:]))
-                square(j)
-                sigmoid(j)
+            if j >= START:
+                back.pop(0)()
+            if START + 1 < j < last:
+                back.pop(0)()
+            if j == last:
+                relu_vector(c, g, slice(0, PACK))
+            else:
+                relu_gpsimd(c, g)
+            if j == 2:
+                interleave_q(3, nc.scalar.copy)
+            if START <= j < last:
+                sigmoid(*divmod(j - START, 2))
+            if j < last:
+                square(c, g, whole)
+
+        c, g = divmod(last, 2)
+        square(c, g, lo)
+        square(c, g, hi)
+        for j in range(last - START, n_units):
+            sigmoid(*divmod(j, 2))
+        for step in back[:-5]:
+            step()
+        product(last - 1)
+        denominator_of(c - 1)
+        codes_b = [quantize_w("b0", w_sq[c, g][:, lo])]
+        invert(str(c - 1))
+        codes_b.append(quantize_w("b1", w_sq[c, g][:, hi]))
+        y_b = y_bank("b", NB)
+        for b in range(NB):
+            multiply(*codes_b[b], y_b[:, b : b + 1])
+        finish_unit(last - 3)
+        denominator("a", y_ps[c][:, :NB])
+        finish_unit(last - 2)
+        invert("a")
+        denominator("b", y_b[:])
+        finish(c, 0, range(NB), y_ps[c], rden["a"][:])
+        invert("b")
+        for b in range(NB):
+            finish(c, g, [b], y_b[:, b : b + 1], rden["b"][:, b : b + 1])

from contextlib import ExitStack
from functools import partial

import concourse.mybir as mybir

H, D, NQ, NT, E = 4, 256, 512, 512, 128
FLOPS = 2 * H * NQ * NT * (D + E)

F32 = mybir.dt.float32
BF16 = mybir.dt.bfloat16
U32 = mybir.dt.uint32
U8 = mybir.dt.uint8
I32 = mybir.dt.int32
FP8X4 = mybir.dt.float8_e4m3fn_x4
ALU = mybir.AluOpType
ACT = mybir.ActivationFunctionType

P = 128
PACK = 4
ROWS = 64
QB = 128
QW = 256
RUN = 4
START = 3
KW = 2 * P
F32_MAX = 3.4028234663852886e38
K_SPLIT = 80


def tile_rows_a_relu2_kb_mask_gate_kernel(tc, qT, kT, t, v, kb, mask, og, out):
    nc = tc.nc
    n_steps = NQ // QW * (H // 2)

    with ExitStack() as ctx:
        sb = ctx.enter_context(tc.tile_pool(name="sb", bufs=1))
        ps = ctx.enter_context(tc.psum_pool(name="ps", bufs=1))
        ctx.enter_context(tc.manual_schedule())

        def tile(shape, dtype, name):
            return sb.tile(shape, dtype, name=name, align_bytes=64)

        def runs_out(x):
            return x.rearrange("p (c i) j -> p c j i", i=RUN)

        def runs_in(x):
            return x.rearrange("p j (c i) -> p c j i", i=RUN)

        def quantize(codes, scales, src):
            nc.vector.quantize_mx(out=codes.bitcast(FP8X4), scales=scales, in_=src)

        t_sb = tile([P, PACK], F32, "t_sb")
        kb_sb = tile([P, PACK], F32, "kb_sb")
        k_raw = tile([ROWS, PACK, NT], F32, "k_raw")
        v_raw = tile([P, PACK, E], F32, "v_raw")
        q_raw = [tile([P, PACK, QW], F32, "q_raw%d" % c) for c in range(4)]
        m_raw = [[tile([P, 2, QW], F32, "m_raw%d_%d" % (c, i)) for i in range(2)] for c in range(2)]
        og_raw = [tile([P, NQ // QB, E], F32, "og_raw%d" % h) for h in range(H)]

        k_src = kT[0].rearrange("(p j) n -> p j n", j=PACK)
        m_src = mask.rearrange("(p r) q -> p r q", r=PACK)

        def load_q(c):
            half, pair = divmod(c, 2)
            src = qT[2 * pair : 2 * pair + 2].rearrange("g (p j) q -> (g p) j q", j=PACK)
            nc.sync.dma_start(out=q_raw[c][:], in_=src[:, :, half * QW : (half + 1) * QW])

        def load_mask(half):
            for i in range(2):
                nc.sync.dma_start(out=m_raw[half][i][:], in_=m_src[:, 2 * i : 2 * i + 2, half * QW : (half + 1) * QW])

        def load_og(h):
            nc.sync.dma_start(out=og_raw[h][:], in_=og[h].rearrange("(c p) e -> p c e", p=P))

        nc.scalar.dma_start(out=k_raw[:], in_=k_src)
        nc.scalar.dma_start(out=kb_sb[:], in_=kb.rearrange("(p r) o -> p (r o)", r=PACK))
        nc.sync.dma_start(out=t_sb[:], in_=t.rearrange("(p r) o -> p (r o)", r=PACK))
        load_q(0)
        load_mask(0)
        load_q(1)

        zero = tile([P, PACK], F32, "zero")
        half_exp = tile([P, PACK], F32, "half_exp")
        t_abs = tile([P, PACK], F32, "t_abs")
        t_sign = tile([P, PACK], F32, "t_sign")
        t_root = tile([P, PACK], F32, "t_root")
        nc.gpsimd.memset(zero[:], 0.0)
        k_mx = [tile([P, KW + KW // PACK], U32, "k_mx%d" % i) for i in range(2)]
        for i in range(2):
            nc.gpsimd.memset(k_mx[i][:, KW:], 0)
        nc.scalar.activation(out=half_exp[:], in_=zero[:], func=ACT.Sigmoid)
        nc.scalar.activation(out=t_abs[:], in_=t_sb[:], func=ACT.Abs)
        nc.scalar.activation(out=t_sign[:], in_=t_sb[:], func=ACT.Sign)
        nc.gpsimd.tensor_tensor(out=t_root[:], in0=t_abs[:], in1=half_exp[:], op=ALU.pow)

        k_il = tile([ROWS, PACK, P, PACK], BF16, "k_il")
        k_codes = [k_mx[r // 2][:, P * (r % 2) : P * (r % 2 + 1)] for r in range(PACK)]
        k_scales = [k_mx[r // 2][:, KW:].bitcast(U8)[:, P * (r % 2) : P * (r % 2 + 1)] for r in range(PACK)]
        k_dst = k_il[:].rearrange("p r s j -> p s j r")
        k_dealt = k_raw[:].rearrange("p j (s r) -> p s j r", r=PACK)
        nc.vector.tensor_copy(out=k_dst[:, :K_SPLIT], in_=k_dealt[:, :K_SPLIT])
        nc.scalar.copy(out=k_dst[:, K_SPLIT:], in_=k_dealt[:, K_SPLIT:])

        def quantize_k(r):
            quantize(k_codes[r][:ROWS], k_scales[r][:ROWS], k_il[:, r].rearrange("p s j -> p (s j)"))

        q_il = [tile([P, QW, PACK], BF16, "q_il%d" % c) for c in range(4)]
        q_codes = [tile([P, QW], U32, "q_codes%d" % c) for c in range(4)]
        q_scales = [tile([P, QW], U8, "q_scales%d" % c) for c in range(4)]

        def quantize_q(c):
            quantize(q_codes[c][:], q_scales[c][:], q_il[c][:].rearrange("p q j -> p (q j)"))

        def interleave_q(c, engine_copy):
            engine_copy(out=runs_out(q_il[c][:]), in_=runs_in(q_raw[c][:]))

        m_root = [tile([P, PACK, QW], F32, "m_root%d" % c) for c in range(2)]

        def scale_mask_scalar(half, rs):
            for r in rs:
                src = m_raw[half][r // 2][:, r % 2]
                nc.scalar.activation(out=m_root[half][:, r], in_=src, func=ACT.Copy, scale=t_root[:, r : r + 1])

        def scale_mask_gpsimd(half):
            for r in range(PACK):
                src = m_raw[half][r // 2][:, r % 2]
                nc.gpsimd.tensor_scalar(
                    out=m_root[half][:, r], in0=src, scalar1=t_root[:, r : r + 1], scalar2=0.0, op0=ALU.mult, op1=ALU.add
                )

        lo, hi = slice(0, QB), slice(QB, QW)
        nc.scalar.copy(out=runs_out(q_il[0][:, hi]), in_=runs_in(q_raw[0][:, :, hi]))
        quantize_k(0)
        quantize_k(1)
        nc.scalar.dma_start(out=k_mx[0][ROWS:].bitcast(I32), in_=k_mx[0][:ROWS].bitcast(I32))
        nc.vector.tensor_copy(out=runs_out(q_il[0][:, lo]), in_=runs_in(q_raw[0][:, :, lo]))
        quantize_k(2)
        quantize_k(3)
        quantize_q(0)
        scale_mask_scalar(0, range(2))
        nc.scalar.dma_start(out=k_mx[1][ROWS:].bitcast(I32), in_=k_mx[1][:ROWS].bitcast(I32))
        scale_mask_scalar(0, range(2, 4))
        load_q(2)
        load_mask(1)
        nc.sync.dma_start(out=v_raw[:], in_=v[0].rearrange("(p r) e -> p r e", r=PACK))
        load_og(0)
        load_q(3)
        for h in range(1, H):
            load_og(h)

        v_il = tile([P, E, PACK], BF16, "v_il")
        v_codes = tile([P, E], U32, "v_codes")
        v_scales = tile([P, E], U8, "v_scales")

        def sign_v():
            sign = t_sign[:].unsqueeze(1).unsqueeze(3).to_broadcast([P, E // RUN, PACK, RUN])
            nc.vector.tensor_tensor(out=runs_out(v_il[:]), in0=runs_in(v_raw[:]), in1=sign, op=ALU.mult)

        banks, lin, pos, w_sq, w_il, y_ps, den, rden, sig, res = ({} for i in range(10))
        NB = QW // QB

        def scores(c, g):
            rows = slice(ROWS * g, ROWS * (g + 1))
            banks[c, g] = []
            for i in range(2):
                bank = ps.tile([P, 2, QW], F32, name="s%d_%d_%d" % (c, g, i), tag="scores%d" % g, bufs=2)
                for r in range(2):
                    banks[c, g].append(bank[:, r])
                    for b in range(NB):
                        cols = slice(QB * b, QB * (b + 1))
                        nc.tensor.matmul_mx(
                            out=bank[:, r, cols],
                            lhsT=k_codes[2 * i + r][rows].bitcast(FP8X4),
                            lhsT_scale=k_scales[2 * i + r][rows],
                            rhs=q_codes[c][rows, cols].bitcast(FP8X4),
                            rhs_scale=q_scales[c][rows, cols],
                            start=True,
                            stop=True,
                        )

        def bias_mask(c, g, r):
            if r == 0:
                lin[c, g] = tile([P, PACK, QW], F32, "lin%d_%d" % (c, g))
                pos[c, g] = tile([P, PACK, QW], F32, "pos%d_%d" % (c, g))
            nc.vector.scalar_tensor_tensor(
                out=lin[c, g][:, r],
                in0=banks[c, g][r],
                scalar=kb_sb[:, r : r + 1],
                in1=m_root[c // 2][:, r],
                op0=ALU.add,
                op1=ALU.mult,
            )

        def relu_gpsimd(c, g):
            nc.gpsimd.tensor_scalar(
                out=pos[c, g][:], in0=lin[c, g][:], scalar1=F32_MAX, scalar2=0.0, op0=ALU.min, op1=ALU.max
            )

        def relu_vector(c, g, rs):
            nc.vector.tensor_scalar_max(out=pos[c, g][:, rs], in0=lin[c, g][:, rs], scalar1=0.0)

        def square(c, g, cols):
            if cols.start == 0:
                w_sq[c, g] = tile([P, QW, PACK], BF16, "w_sq%d_%d" % (c, g))
            nc.scalar.activation(out=runs_out(w_sq[c, g][:, cols]), in_=runs_in(pos[c, g][:, :, cols]), func=ACT.Square)

        def second_product(name, w, y):
            multiply(*quantize_w(name, w), y)

        def quantize_w(name, w):
            width = w.shape[1]
            codes = tile([P, width], U32, "w_codes" + name)
            scales = tile([P, width], U8, "w_scales" + name)
            quantize(codes[:], scales[:], w.rearrange("p q r -> p (q r)"))
            return codes, scales

        def multiply(codes, scales, y):
            for b in range(y.shape[1]):
                cols = slice(QB * b, QB * (b + 1))
                nc.tensor.matmul_mx(
                    out=y[:, b],
                    lhsT=codes[:, cols].bitcast(FP8X4),
                    lhsT_scale=scales[:, cols],
                    rhs=v_codes[:].bitcast(FP8X4),
                    rhs_scale=v_scales[:],
                    start=True,
                    stop=True,
                )

        def sigmoid(c, g):
            h, half = 2 * (c % 2) + g, c // 2
            sig[c, g] = tile([P, NB, E], F32, "sig%d_%d" % (c, g))
            nc.scalar.activation(out=sig[c, g][:], in_=og_raw[h][:, NB * half : NB * (half + 1)], func=ACT.Sigmoid)

        def denominator(name, y):
            den[name] = tile([P, y.shape[1]], F32, "den" + name)
            nc.vector.tensor_scalar_add(out=den[name][:], in0=y[:, :, E - 1], scalar1=1.0)

        def denominator_of(c):
            denominator(str(c), y_ps[c][:])

        def invert(name):
            rden[name] = tile([P, den[name].shape[1]], F32, "rden" + name)
            nc.vector.reciprocal(out=rden[name][:], in_=den[name][:])

        def finish(c, g, blocks, y, inv):
            h, q0 = 2 * (c % 2) + g, (c // 2) * QW + blocks[0] * QB
            result = tile([P, len(blocks), E], F32, "res%d_%d_%d" % (c, g, blocks[0]))
            for i, b in enumerate(blocks):
                nc.vector.scalar_tensor_tensor(
                    out=result[:, i], in0=y[:, i], scalar=inv[:, i : i + 1], in1=sig[c, g][:, b], op0=ALU.mult, op1=ALU.mult
                )
            dst = out[h, q0 : q0 + len(blocks) * QB].rearrange("(c p) e -> p c e", p=P)
            nc.sync.dma_start(out=dst, in_=result[:])

        def y_bank(name, blocks):
            return ps.tile([P, blocks, E], F32, name="y" + name, tag="y", bufs=4)

        whole = slice(0, QW)
        n_units = 2 * n_steps
        last = n_units - 1

        def product(j):
            c, g = divmod(j, 2)
            if g == 0:
                y_ps[c] = y_bank(str(c), 2 * NB)
            second_product(str(j), w_sq[c, g][:], y_ps[c][:, NB * g : NB * (g + 1)])

        def finish_unit(j):
            c, g = divmod(j, 2)
            finish(c, g, range(NB), y_ps[c][:, NB * g : NB * (g + 1)], rden[str(c)][:, NB * g : NB * (g + 1)])

        back = [partial(product, 0), partial(product, 1)]
        for c in range(n_steps - 1):
            back.append(partial(denominator_of, c))
            back.append(partial(product, 2 * c + 2))
            back.append(partial(invert, str(c)))
            if 2 * c + 3 < last:
                back.append(partial(product, 2 * c + 3))
            back.append(partial(finish_unit, 2 * c))
            back.append(partial(finish_unit, 2 * c + 1))

        scores(0, 0)
        interleave_q(1, nc.scalar.copy)
        interleave_q(2, nc.scalar.copy)
        scale_mask_scalar(1, range(PACK))
        for j in range(n_units):
            c, g = divmod(j, 2)
            if j < last:
                scores(*divmod(j + 1, 2))
            bias_mask(c, g, 0)
            bias_mask(c, g, 1)
            bias_mask(c, g, 2)
            if j == last:
                back.pop(0)()
            bias_mask(c, g, 3)
            if g == 0 and c + 1 < n_steps:
                quantize_q(c + 1)
            if j == 2:
                sign_v()
            if j == START:
                quantize(v_codes[:], v_scales[:], v_il[:].rearrange("p e r -> p (e r)"))
            if j >= START:
                back.pop(0)()
            if START + 1 < j < last:
                back.pop(0)()
            if j == last:
                relu_vector(c, g, slice(0, PACK))
            else:
                relu_gpsimd(c, g)
            if j == 2:
                interleave_q(3, nc.scalar.copy)
            if START <= j < last:
                sigmoid(*divmod(j - START, 2))
            if j < last:
                square(c, g, whole)

        c, g = divmod(last, 2)
        square(c, g, lo)
        square(c, g, hi)
        for j in range(last - START, n_units):
            sigmoid(*divmod(j, 2))
        for step in back[:-5]:
            step()
        product(last - 1)
        denominator_of(c - 1)
        codes_b = [quantize_w("b0", w_sq[c, g][:, lo])]
        invert(str(c - 1))
        codes_b.append(quantize_w("b1", w_sq[c, g][:, hi]))
        y_b = y_bank("b", NB)
        for b in range(NB):
            multiply(*codes_b[b], y_b[:, b : b + 1])
        finish_unit(last - 3)
        denominator("a", y_ps[c][:, :NB])
        finish_unit(last - 2)
        invert("a")
        denominator("b", y_b[:])
        finish(c, 0, range(NB), y_ps[c], rden["a"][:])
        invert("b")
        for b in range(NB):
            finish(c, g, [b], y_b[:, b : b + 1], rden["b"][:, b : b + 1])
